import numpy as np
CORES = [2,10,18,26,34,42,50,58,130,138,146,154,162,170,178,186]
N = 16
ROUNDS, ROOT = 8, 5
def setup_inputs(rng):
    return {"x": rng.standard_normal((N, ROUNDS, 128, 128), dtype=np.float32)}
def reference(x):
    y = np.full(x.shape, np.nan, x.dtype)
    y[ROOT] = x.sum(axis=0, dtype=np.float64).astype(x.dtype)
    return {"y": y}

from concourse.bass import DstId, RemoteDMATransfer
from concourse.mybir import AluOpType

ROWS = 640
UNIT = 64
LEVELS = 7
SCRATCH = {"buf": ("dram", [2 * ROWS, 64], "float32")}
SEMAPHORES = (["loaded", "sent", "csent"] + ["a%d%d" % (g, l) for g in range(2) for l in range(1, LEVELS + 1)]
              + ["cr%d" % l for l in range(1, LEVELS + 1)])


def core_of(h, c):
    return 128 * h + 8 * c + 2


ROOTC, FOUR = core_of(0, 5), core_of(0, 4)
E0 = [core_of(0, c) for c in (0, 2, 6)]
O0 = [c + 8 for c in E0]
E1 = [core_of(1, c) for c in (0, 2, 4, 6)]
O1 = [c + 8 for c in E1]
EVEN = E0 + E1 + [FOUR]


def stage_rows(c):
    return 256 if c == FOUR else 128


def build_gen(base):
    A, B = base, base + 256
    lg = []
    for j, e in enumerate(E1):
        lg.append((1, FOUR, e, A + 64 * j, A + 64 * j + 64))
        r = j // 2
        lg.append((1, e, e + 8, A + 128 * (1 - r), A + 128 * (1 - r) + 128))
        lg.append((2, e, e + 8, A + 128 * r, A + 128 * r + 128))
    for e in E0:
        lg += [(1, e, e + 8, A, A + 128), (2, e, e + 8, A + 128, A + 256)]
    for o in O0 + O1:
        lg += [(1, o, o - 8, B, B + 128), (2, o, o - 8, B + 128, B + 256)]
    for H, P0, P1, sink in ((A, O0, O1, ROOTC), (B, E0, E1, FOUR)):
        for i in range(4):
            lg += [(3, P1[i], P1[j], H + 64 * j, H + 64 * j + 64) for j in range(4) if j != i]
            lg.append((4, P1[i], P0[0] if i < 2 else P0[2], H + 64 * i, H + 64 * i + 64))
        lg += [(3, P0[2], P0[0], H, H + 128), (3, P0[0], P0[2], H + 128, H + 256)]
        lg += [(5, P0[0], P0[1], H, H + 128), (5, P0[2], P0[1], H + 128, H + 256)]
        lg.append((6, P0[1], sink, H, H + 256))
    lg.append((7, FOUR, ROOTC, B, B + 256))
    lg.sort(key=lambda m: m[0])

    def staged(c, row):
        return c != ROOTC and ((row < B) if c in EVEN else (row >= B))

    msgs, covered, bump = [], {}, {}
    for l, s, d, a, b in lg:
        for a1 in range(a, b, UNIT):
            if staged(s, a1):
                lo = A if s == FOUR else (a1 // 128) * 128
                srcs = [ROWS - stage_rows(s) + a1 - lo]
            else:
                assert a1 in covered[s]
                srcs = [a1 - (B if s in EVEN else A)]
            for m in msgs:
                if m["d"] == s and not m["al"] and m["a"] == a1:
                    assert m["l"] < l
                    srcs.append(m["to"])
            cov = covered.setdefault(d, set())
            al = not staged(d, a1) and a1 not in cov
            if al:
                cov.add(a1)
                to = a1 - (base if d == ROOTC else (B if d in EVEN else A))
            else:
                to = bump.get(d, 256)
                bump[d] = to + UNIT
                assert d != ROOTC and bump[d] <= ROWS - stage_rows(d)
            msgs.append(dict(l=l, s=s, d=d, a=a1, to=to, srcs=srcs, al=al, st=staged(s, a1)))
    return msgs


PLAN = [build_gen(0), build_gen(512)]


def rank_program(g, core, T, topo):
    if T.rank_of(core) is None:
        return
    S = T.sem
    sems = dict(zip(SEMAPHORES, [S.loaded, S.sent, S.csent,
                                 S.a01, S.a02, S.a03, S.a04, S.a05, S.a06, S.a07,
                                 S.a11, S.a12, S.a13, S.a14, S.a15, S.a16, S.a17,
                                 S.cr1, S.cr2, S.cr3, S.cr4, S.cr5, S.cr6, S.cr7]))
    cnt = {"loaded": 0, "sent": 0}

    def rows(r, n):
        return T.buf[2 * r:2 * (r + n), :]

    def local(out, in_, add=False):
        if add:
            g.dma_start(out=out, in_=in_, accum_op=AluOpType.add).then_inc(S.loaded, 16)
        else:
            g.dma_start(out=out, in_=in_).then_inc(S.loaded, 16)
        cnt["loaded"] += 16
        g.wait_ge(S.loaded, cnt["loaded"])

    def rounds(t, a, n):
        return t[a // 128] if n == 128 else t[a // 128:(a + n) // 128]

    def dst(d):
        rid, pid = topo.addr(d, core)
        return DstId(rid=rid, pnc=pid)

    if core == ROOTC:
        local(T.y[:], T.x[:])
    for gen, msgs in enumerate(PLAN):
        base = 512 * gen
        mine = [m for m in msgs if m["s"] == core]
        inc = [m for m in msgs if m["d"] == core]
        waited = 0
        need_acc = core != ROOTC

        def wait_to(level, waited):
            for l in range(waited + 1, level):
                n = sum(1 for m in inc if m["l"] == l)
                if n:
                    g.wait_ge(sems["a%d%d" % (gen, l)], n)
            return max(waited, level - 1)

        for l in range(1, LEVELS + 1):
            out = [m for m in mine if m["l"] == l]
            if not out:
                continue
            waited = wait_to(l, waited)
            if out[0]["st"]:
                if cnt["sent"]:
                    g.wait_ge(S.sent, cnt["sent"])
                n = stage_rows(core)
                local(rows(ROWS - n, n), rounds(T.x, (out[0]["a"] // n) * n, n))
            elif need_acc:
                assert max(m["l"] for m in inc if m["al"]) < l
                local(rows(0, 256), rounds(T.x, base + (256 if core in EVEN else 0), 256), add=True)
                need_acc = False
            if gen == 1:
                first = {}
                for m in mine:
                    first[m["d"]] = min(first.get(m["d"], 99), m["l"])
                n = sum(1 for v in first.values() if v == l)
                if n:
                    g.wait_ge(sems["cr%d" % l], n)
            trs = []
            for i, m in enumerate(out):
                srcs = [rows(r, UNIT) for r in m["srcs"]]
                kw = dict(src=srcs[0], dst=rows(m["to"], UNIT)) if len(srcs) == 1 else \
                    dict(srcs=srcs, dsts=[rows(m["to"], UNIT)], alu_op=1)
                trs.append(RemoteDMATransfer(dst_ids=[dst(m["d"])], dma_engine_mask=1 << i,
                                             remote_sem=sems["a%d%d" % (gen, l)], **kw))
            g.remote_dma_fused(trs, local_sem=S.sent)
            cnt["sent"] += len(trs)
        wait_to(LEVELS + 1, waited)
        if core == ROOTC:
            for h in (0, 256):
                local(rounds(T.y, base + h, 256), rows(h, 256), add=True)
        else:
            g.wait_ge(S.sent, cnt["sent"])
        if gen == 0:
            first = {}
            for m in PLAN[1]:
                if m["d"] == core:
                    first[m["s"]] = min(first.get(m["s"], 99), m["l"])
            trs = [RemoteDMATransfer(dst_ids=[dst(s)], dma_engine_mask=1 << i, remote_sem=sems["cr%d" % l])
                   for i, (s, l) in enumerate(sorted(first.items()))]
            if trs:
                g.remote_dma_fused(trs, local_sem=S.csent)
                g.wait_ge(S.csent, len(trs))
